import numpy as np
import ml_dtypes


def mxq(x, axis, fmt="e4m3"):
    dtype, down = {"e4m3": (ml_dtypes.float8_e4m3fn, 7), "e5m2": (ml_dtypes.float8_e5m2, 14)}[fmt]
    v = np.moveaxis(np.asarray(x, np.float32).astype(ml_dtypes.bfloat16).astype(np.float64), axis, -1)
    blocks = v.reshape(v.shape[:-1] + (-1, 32))
    amax = np.abs(blocks).max(-1, keepdims=True)
    byte = np.maximum(np.where(amax > 0, np.frexp(amax)[1] - 1 + 127, 0) - down, 1)
    scale = np.exp2(byte - 127.0)
    codes = (blocks / scale).astype(np.float32).astype(dtype).astype(np.float64)
    return np.moveaxis((codes * scale).reshape(v.shape), -1, axis)


WIDE = False


def mx_kscale(k):
    if not WIDE:
        return np.ones(k)
    levels = np.array([10, -10, 5, -5, 0])
    if k % 512:
        return np.exp2(np.random.permutation(np.resize(levels, k // 32))).repeat(32)
    a = np.empty((k // 512, 16))
    for p in range(k // 512):
        a[p, :8] = np.random.permutation(np.resize(levels, 8))
        for g in range(8):
            far = levels[np.abs(levels - a[p, g]) >= 10]
            a[p, g + 8] = far[np.random.randint(len(far))]
    return np.exp2(a.ravel()).repeat(32)


def f64(x):
    return np.asarray(x).astype(np.float64)


def striped(idx):
    return np.tile(np.asarray(idx).reshape(-1, 16).T, (8, 1)).astype(np.uint16)


def unstriped(offs):
    return offs[:16].T.reshape(-1).astype(np.int64)


E2M1 = np.array([0.0, 0.5, 1.0, 1.5, 2.0, 3.0, 4.0, 6.0, -0.0, -0.5, -1.0, -1.5, -2.0, -3.0, -4.0, -6.0])


def pack_weight(w, fmt):
    k, n = w.shape
    w = f64(np.asarray(w, np.float32).astype(ml_dtypes.bfloat16)).reshape(k // 32, 32, n)
    amax = np.abs(w).max(1)
    if fmt == "e4m3":
        byte = np.frexp(amax)[1] - 1 + 127 - 7
    else:
        mant, ex = np.frexp(amax / 6.0)
        byte = np.where(mant > 0.5, ex, ex - 1) + 127
    byte = np.clip(np.where(amax > 0, byte, 1), 1, 254)
    scaled = (w * np.exp2(127.0 - byte)[:, None, :]).reshape(k, n).astype(np.float32)
    by_word = np.ascontiguousarray(scaled.reshape(k // 512, 128, 4, n).transpose(0, 1, 3, 2))
    if fmt == "e4m3":
        words = by_word.astype(ml_dtypes.float8_e4m3fn).view(np.uint8)
    else:
        c = by_word.astype(ml_dtypes.float4_e2m1fn).view(np.uint8) & 0xF
        words = (c[..., 0::2] | (c[..., 1::2] << 4)).reshape(k // 512, 128, 2 * n)
    return np.ascontiguousarray(words), np.ascontiguousarray(byte.astype(np.uint8).reshape(k // 512, 16, n))


def unpack_weight(words, scales, fmt):
    g, _, n = scales.shape
    words = np.ascontiguousarray(words).reshape(g, 128, n, -1)
    if fmt == "e4m3":
        vals = words.view(ml_dtypes.float8_e4m3fn).astype(np.float64)
    else:
        nib = np.empty((g, 128, n, 4), np.uint8)
        nib[..., 0::2] = words & 0xF
        nib[..., 1::2] = words >> 4
        vals = E2M1[nib]
    vals = vals * np.repeat(np.exp2(scales.astype(np.float64) - 127.0), 8, axis=1)[..., None]
    return vals.transpose(0, 1, 3, 2).reshape(g * 512, n)


def softplus(v):
    return np.log(1.0 + np.exp(v))


def sigmoid(v):
    return 1.0 / (1.0 + np.exp(-v))


D, T, U, I, J, G = 512, 1024, 1024, 256, 512, 128


def setup_inputs():
    n = np.random.standard_normal
    idx = np.random.permutation(T)[:I]
    idx2 = np.random.permutation(U)[:J]
    fd = mx_kscale(D)
    tabbp = pack_weight(n((D, U)) / fd[:, None], "e2m1")
    return {
        "taba": (n((D, T)) * 1 / np.sqrt(D) * fd[:, None]).astype(np.float32),
        "dtab": (n((D, T)) * 1.3 / np.sqrt(D) * fd[:, None]).astype(np.float32),
        "tabb_words": tabbp[0],
        "tabb_scales": tabbp[1],
        "stake": (n((I, G)) * 4.0).astype(np.float32),
        "bias": (np.random.uniform(0.0, 2.0, (1, J))).astype(np.float32),
        "base": (0.3 * n((I, J))).astype(np.float32),
        "offs": striped(idx),
        "offs2": striped(idx2),
    }


def reference(taba, dtab, tabb_words, tabb_scales, stake, bias, base, offs, offs2):
    idx = unstriped(offs)
    idx2 = unstriped(offs2)
    tabbu = unpack_weight(tabb_words, tabb_scales, "e2m1")
    tabaidxq = mxq(f64(taba)[:, idx], 0, "e4m3")
    tabbidx2g = tabbu[:, idx2]
    s = tabaidxq.T @ tabbidx2g
    dtabidxq = mxq(f64(dtab)[:, idx], 0, "e4m3")
    ts = dtabidxq.T @ tabbidx2g
    u1 = softplus((s + f64(bias)) * (-1.0))
    ch = np.exp(u1.reshape(I, G, J // G).sum(axis=2) * (-1.0))
    dch = f64(stake) / (ch + 1.0)
    e1 = dch * ch * (-1.0)
    r1 = np.repeat(e1, J // G, axis=1)
    xu1 = ts * (-1.0) * sigmoid((s + f64(bias)) * (-1.0))
    xch = xu1.reshape(I, G, J // G).sum(axis=2) * (-1.0) * ch
    xdch = xch * f64(stake) / np.square(ch + 1.0) * (-1.0)
    xe1 = (xdch * ch + xch * dch) * (-1.0)
    xr1 = np.repeat(xe1, J // G, axis=1)
    xds = (xr1 * sigmoid((s + f64(bias)) * (-1.0)) + ts * (-1.0) * sigmoid((s + f64(bias)) * (-1.0)) * (1.0 - sigmoid((s + f64(bias)) * (-1.0))) * r1) * (-1.0)
    y = xds + f64(base)
    return y

@@ -1,0 +1,228 @@
+from contextlib import ExitStack
+
+import concourse.mybir as mybir
+from concourse.masks import make_identity
+
+F32 = mybir.dt.float32
+BF16 = mybir.dt.bfloat16
+I32 = mybir.dt.int32
+U32 = mybir.dt.uint32
+U16 = mybir.dt.uint16
+U8 = mybir.dt.uint8
+FP8X4 = mybir.dt.float8_e4m3fn_x4
+FP4X4 = mybir.dt.float4_e2m1fn_x4
+ACT = mybir.ActivationFunctionType
+ALU = mybir.AluOpType
+
+P = 128
+D, T, U, I, J, G = 512, 1024, 1024, 256, 512, 128
+PACK = 4
+TEAM = 4
+HALVES = 2
+
+FLOPS = 2 * 2 * D * I * J
+
+
+def tile_attend_hvpairteams_kernel(tc, taba, dtab, tabb_words, tabb_scales, stake, bias, base, offs, offs2, out):
+    nc = tc.nc
+    with ExitStack() as ctx:
+        sb = ctx.enter_context(tc.tile_pool(name="sb", bufs=1))
+        ps = ctx.enter_context(tc.psum_pool(name="ps", bufs=1))
+
+        first_list = sb.tile([P, I // 16], U16, name="first_list")
+        second_list = sb.tile([P, J // 16], U16, name="second_list")
+        words = sb.tile([P, U], U16, name="words")
+        scale_rows = sb.tile([P, U], U8, name="scale_rows")
+        a_planes = [sb.tile([P, T], F32, name="a_plane%d" % t) for t in range(PACK)]
+        d_planes = [sb.tile([P, T], F32, name="d_plane%d" % t) for t in range(PACK)]
+        bias_sb = sb.tile([P, TEAM], F32, name="bias_sb")
+        stake_sb = sb.tile([P, HALVES, G], F32, name="stake_sb")
+        base_sb = [sb.tile([P, J], F32, name="base_sb%d" % h) for h in range(HALVES)]
+        ident = sb.tile([P, P], F32, name="ident")
+        warm = sb.tile([P, 2], F32, name="warm")
+
+        nc.gpsimd.memset(scale_rows[:].bitcast(I32), 0)
+        make_identity(nc, ident[:])
+        nc.vector.memset(warm[:, 0:1], 0.0)
+        nc.scalar.activation(out=warm[:, 1:2], in_=warm[:, 0:1], func=ACT.Sigmoid)
+
+        nc.sync.dma_start(second_list[:], offs2)
+        nc.sync.dma_start(out=words[:].bitcast(I32), in_=tabb_words[0].bitcast(I32))
+        nc.sync.dma_start(first_list[:], offs)
+        a_rows = taba.rearrange("(p t) c -> p t c", t=PACK)
+        d_rows = dtab.rearrange("(p t) c -> p t c", t=PACK)
+        nc.sync.dma_start(out=a_planes[0][:], in_=a_rows[:, 0, :])
+        for quad in range(4):
+            nc.sync.dma_start(
+                out=scale_rows[32 * quad : 32 * quad + 4, :].bitcast(I32),
+                in_=tabb_scales[0, 4 * quad : 4 * quad + 4, :].bitcast(I32),
+            )
+        for t in range(1, PACK):
+            nc.sync.dma_start(out=a_planes[t][:], in_=a_rows[:, t, :])
+        nc.sync.dma_start(out=bias_sb[:], in_=bias.rearrange("o (p r) -> p (o r)", r=TEAM))
+        nc.sync.dma_start(out=stake_sb[:], in_=stake.rearrange("(h p) g -> p h g", p=P))
+        for t in range(PACK):
+            nc.sync.dma_start(out=d_planes[t][:], in_=d_rows[:, t, :])
+        for h in range(HALVES):
+            nc.sync.dma_start(out=base_sb[h][:], in_=base[h * P : (h + 1) * P, :])
+
+        words_picked = sb.tile([P, J], U16, name="words_picked")
+        scales_picked = sb.tile([P, J], U8, name="scales_picked")
+        b_words = sb.tile([P, J], U16, name="b_words", align_bytes=64)
+        b_scales = sb.tile([P, J], U8, name="b_scales", align_bytes=64)
+        nc.vector.tensor_copy(words_picked[:], words[:].indirect(second_list[:]))
+        nc.vector.tensor_copy(
+            out=b_words[:].rearrange("p (r c g) -> p c r g", r=TEAM, g=8),
+            in_=words_picked[:].rearrange("p (c g r) -> p c r g", r=TEAM, g=8),
+        )
+        nc.vector.tensor_copy(scales_picked[:], scale_rows[:].indirect(second_list[:]))
+        nc.vector.tensor_copy(
+            out=b_scales[:].rearrange("p (r c g) -> p c r g", r=TEAM, g=16),
+            in_=scales_picked[:].rearrange("p (c g r) -> p c r g", r=TEAM, g=16),
+        )
+
+        def operand_tiles(tag):
+            woven = sb.tile([P, I, PACK], BF16, name=tag + "_woven", align_bytes=64)
+            codes = sb.tile([P, I], U32, name=tag + "_codes", align_bytes=64)
+            scales = sb.tile([P, I], U8, name=tag + "_scales", align_bytes=64)
+            return woven, codes, scales
+
+        def quantise(woven, codes, scales, cols):
+            nc.vector.quantize_mx(
+                out=codes[:, cols].bitcast(FP8X4),
+                scales=scales[:, cols],
+                in_=woven[:, cols, :].rearrange("p i t -> p (i t)"),
+            )
+
+        def scores(dst, r, codes, scales, cols):
+            member = slice(r * P, (r + 1) * P)
+            nc.tensor.matmul_mx(
+                out=dst,
+                lhsT=b_words[:, member].bitcast(FP4X4),
+                lhsT_scale=b_scales[:, member],
+                rhs=codes[:, cols].bitcast(FP8X4),
+                rhs_scale=scales[:, cols],
+                start=True,
+                stop=True,
+            )
+
+        a_woven, a_codes, a_scales = operand_tiles("a")
+        for t in range(2):
+            rounded = sb.tile([P, T], BF16, name="a_rounded%d" % t)
+            nc.scalar.activation(out=rounded[:], in_=a_planes[t][:], func=ACT.Copy)
+            nc.scalar.activation(out=a_woven[:, :, t], in_=rounded[:].indirect(first_list[:]), func=ACT.Copy)
+        for t in range(2, PACK):
+            nc.vector.tensor_copy(a_woven[:, :, t], a_planes[t][:].indirect(first_list[:]))
+        quantise(a_woven, a_codes, a_scales, slice(0, I))
+        s_ps = [ps.tile([P, 2, I], F32, name="s_ps%d" % b, tag="bank%d" % b) for b in range(2)]
+        prob = sb.tile([P, TEAM, I], F32, name="prob")
+        for r in range(TEAM):
+            scores(s_ps[r // 2][:, r % 2, :], r, a_codes, a_scales, slice(0, I))
+        for r in range(TEAM):
+            nc.scalar.activation(
+                out=prob[:, r, :], in_=s_ps[r // 2][:, r % 2, :], func=ACT.Sigmoid, bias=bias_sb[:, r : r + 1]
+            )
+
+        d_woven, d_codes, d_scales = operand_tiles("d")
+        for t in range(PACK - 1):
+            nc.vector.tensor_copy(d_woven[:, :, t], d_planes[t][:].indirect(first_list[:]))
+
+        stake_ps = ps.tile([P, HALVES, P], F32, name="stake_ps", tag="bank4")
+        for h in range(HALVES):
+            nc.tensor.transpose(stake_ps[:, h, :], stake_sb[:, h, :], ident[:])
+
+        pairs = sb.tile([P, 2, I], F32, name="pairs")
+        chance = sb.tile([P, I], F32, name="chance")
+        root = sb.tile([P, I], F32, name="root")
+        recip = sb.tile([P, I], F32, name="recip")
+        recip_sq = sb.tile([P, I], F32, name="recip_sq")
+        staked = sb.tile([P, I], F32, name="staked")
+        weight = sb.tile([P, I], F32, name="weight")
+        weight2 = sb.tile([P, I], F32, name="weight2")
+        nc.vector.tensor_tensor(pairs[:], prob[:, 0:2, :], prob[:, 2:4, :], ALU.mult)
+        nc.vector.tensor_tensor(chance[:], pairs[:, 0, :], pairs[:, 1, :], ALU.mult)
+        nc.scalar.activation(out=root[:], in_=chance[:], func=ACT.Abs_reciprocal_sqrt, bias=1.0)
+        nc.scalar.activation(out=recip[:], in_=root[:], func=ACT.Square)
+        nc.scalar.activation(out=recip_sq[:], in_=recip[:], func=ACT.Square)
+        nc.vector.tensor_tensor(staked[:], stake_ps[:].rearrange("p h i -> p (h i)"), chance[:], ALU.mult)
+        ts_ps = [ps.tile([P, TEAM, P], F32, name="ts_ps%d" % h, tag="bank%d" % (2 + h)) for h in range(HALVES)]
+        for h in range(HALVES):
+            cols = slice(h * P, (h + 1) * P)
+            entries = first_list[:, h * (P // 16) : (h + 1) * (P // 16)]
+            nc.vector.tensor_copy(d_woven[:, cols, PACK - 1], d_planes[PACK - 1][:].indirect(entries))
+        for h in range(HALVES):
+            cols = slice(h * P, (h + 1) * P)
+            quantise(d_woven, d_codes, d_scales, cols)
+            for r in range(TEAM):
+                scores(ts_ps[h][:, r, :], r, d_codes, d_scales, cols)
+        nc.vector.tensor_tensor(weight[:], staked[:], recip[:], ALU.mult)
+        nc.vector.tensor_tensor(weight2[:], staked[:], recip_sq[:], ALU.mult)
+
+        moved = []
+        sums_back = []
+        for h in range(HALVES):
+            cols = slice(h * P, (h + 1) * P)
+            moved.append(sb.tile([P, TEAM, P], F32, name="moved%d" % h))
+            nc.vector.scalar_tensor_tensor(
+                out=moved[h][:], in0=prob[:, :, cols], scalar=1.0, in1=ts_ps[h][:], op0=ALU.subtract, op1=ALU.mult
+            )
+            sums_ps = ps.tile([P, P], F32, name="sums_ps%d" % h, tag="bank%d" % (5 + h))
+            for r in range(TEAM):
+                nc.tensor.matmul(
+                    sums_ps[:], lhsT=moved[h][:, r, :], rhs=ident[:], is_transpose=True, start=r == 0, stop=r == TEAM - 1
+                )
+            sums_sb = sb.tile([P, P], F32, name="sums_sb%d" % h)
+            nc.scalar.copy(out=sums_sb[:], in_=sums_ps[:])
+            sums_back.append(ps.tile([P, P], F32, name="sums_back%d" % h, tag="bank%d" % (7 if h == 0 else 4)))
+            nc.tensor.transpose(sums_back[h][:], sums_sb[:], ident[:])
+
+        curved = []
+        for h in range(HALVES):
+            curved.append(sb.tile([P, TEAM, P], F32, name="curved%d" % h))
+            nc.vector.tensor_tensor(curved[h][:], moved[h][:], prob[:, :, h * P : (h + 1) * P], ALU.mult)
+        out_ps = []
+        for h in range(HALVES):
+            cols = slice(h * P, (h + 1) * P)
+            own = sb.tile([P, TEAM, P], F32, name="own%d" % h)
+            nc.vector.tensor_tensor(
+                own[:], curved[h][:], weight[:, cols].unsqueeze(1).to_broadcast([P, TEAM, P]), ALU.mult
+            )
+            out_ps.append(ps.tile([P, TEAM, G], F32, name="out_ps%d" % h, tag="bank%d" % h))
+            for r in range(TEAM):
+                nc.tensor.matmul(
+                    out_ps[h][:, r, :], lhsT=own[:, r, :], rhs=ident[:], is_transpose=True, start=r == 0, stop=False
+                )
+        team_terms = []
+        for h in range(HALVES):
+            cols = slice(h * P, (h + 1) * P)
+            team_terms.append(sb.tile([P, P], F32, name="team_term%d" % h))
+            nc.vector.tensor_tensor(team_terms[h][:], sums_back[h][:], weight2[:, cols], ALU.mult)
+        for h in range(HALVES):
+            cols = slice(h * P, (h + 1) * P)
+            shared = sb.tile([P, TEAM, P], F32, name="shared%d" % h)
+            nc.vector.scalar_tensor_tensor(
+                out=shared[:],
+                in0=prob[:, :, cols],
+                scalar=1.0,
+                in1=team_terms[h][:].unsqueeze(1).to_broadcast([P, TEAM, P]),
+                op0=ALU.subtract,
+                op1=ALU.mult,
+            )
+            for r in range(TEAM):
+                nc.tensor.matmul(
+                    out_ps[h][:, r, :],
+                    lhsT=shared[:, r, :],
+                    rhs=ident[:],
+                    is_transpose=True,
+                    start=False,
+                    stop=r == TEAM - 1,
+                )
+        for h in range(HALVES):
+            result = sb.tile([P, J], F32, name="result%d" % h)
+            nc.vector.tensor_tensor(
+                result[:].rearrange("p (g r) -> p g r", r=TEAM),
+                out_ps[h][:].rearrange("p r g -> p g r"),
+                base_sb[h][:].rearrange("p (g r) -> p g r", r=TEAM),
+                ALU.add,
+            )
+            nc.sync.dma_start(out=out[h * P : (h + 1) * P, :], in_=result[:])

@@ -46,23 +46,26 @@ def tile_attend_hvpairteams_kernel(tc, taba, dtab, tabb_words, tabb_scales, stak
         nc.vector.memset(warm[:, 0:1], 0.0)
         nc.scalar.activation(out=warm[:, 1:2], in_=warm[:, 0:1], func=ACT.Sigmoid)
 
+        a_rows = taba.rearrange("(p t) c -> p t c", t=PACK)
+        d_rows = dtab.rearrange("(p t) c -> p t c", t=PACK)
         nc.sync.dma_start(second_list[:], offs2)
         nc.sync.dma_start(out=words[:].bitcast(I32), in_=tabb_words[0].bitcast(I32))
         nc.sync.dma_start(first_list[:], offs)
-        a_rows = taba.rearrange("(p t) c -> p t c", t=PACK)
-        d_rows = dtab.rearrange("(p t) c -> p t c", t=PACK)
         nc.sync.dma_start(out=a_planes[0][:], in_=a_rows[:, 0, :])
         for quad in range(4):
             nc.sync.dma_start(
                 out=scale_rows[32 * quad : 32 * quad + 4, :].bitcast(I32),
                 in_=tabb_scales[0, 4 * quad : 4 * quad + 4, :].bitcast(I32),
             )
-        for t in range(1, PACK):
-            nc.sync.dma_start(out=a_planes[t][:], in_=a_rows[:, t, :])
+        nc.sync.dma_start(out=a_planes[1][:], in_=a_rows[:, 1, :])
+        nc.sync.dma_start(out=a_planes[2][:], in_=a_rows[:, 2, :])
+        nc.sync.dma_start(out=a_planes[3][:], in_=a_rows[:, 3, :])
         nc.sync.dma_start(out=bias_sb[:], in_=bias.rearrange("o (p r) -> p (o r)", r=TEAM))
+        nc.sync.dma_start(out=d_planes[0][:], in_=d_rows[:, 0, :])
+        nc.sync.dma_start(out=d_planes[1][:], in_=d_rows[:, 1, :])
         nc.sync.dma_start(out=stake_sb[:], in_=stake.rearrange("(h p) g -> p h g", p=P))
-        for t in range(PACK):
-            nc.sync.dma_start(out=d_planes[t][:], in_=d_rows[:, t, :])
+        nc.sync.dma_start(out=d_planes[2][:], in_=d_rows[:, 2, :])
+        nc.sync.dma_start(out=d_planes[3][:], in_=d_rows[:, 3, :])
         for h in range(HALVES):
             nc.sync.dma_start(out=base_sb[h][:], in_=base[h * P : (h + 1) * P, :])
 
@@ -82,10 +85,16 @@ def tile_attend_hvpairteams_kernel(tc, taba, dtab, tabb_words, tabb_scales, stak
         )
 
         def operand_tiles(tag):
-            woven = sb.tile([P, I, PACK], BF16, name=tag + "_woven", align_bytes=64)
-            codes = sb.tile([P, I], U32, name=tag + "_codes", align_bytes=64)
+            woven = sb.tile([P, I, PACK], BF16, name=tag + "_woven", tag=tag + "_woven", align_bytes=64)
+            codes = sb.tile([P, I], U32, name=tag + "_codes", tag=tag + "_codes", align_bytes=64)
             scales = sb.tile([P, I], U8, name=tag + "_scales", align_bytes=64)
             return woven, codes, scales
+
+        def weave(copy, picked, woven, cols):
+            copy(
+                out=woven[:, cols, :].rearrange("p (c i) t -> p c t i", i=4),
+                in_=picked[:, :, cols].rearrange("p t (c i) -> p c t i", i=4),
+            )
 
         def quantise(woven, codes, scales, cols):
             nc.vector.quantize_mx(
@@ -107,13 +116,20 @@ def tile_attend_hvpairteams_kernel(tc, taba, dtab, tabb_words, tabb_scales, stak
             )
 
         a_woven, a_codes, a_scales = operand_tiles("a")
+        picked = sb.tile([P, PACK, I], BF16, name="picked")
+        a_picked = picked
         for t in range(2):
             rounded = sb.tile([P, T], BF16, name="a_rounded%d" % t)
             nc.scalar.activation(out=rounded[:], in_=a_planes[t][:], func=ACT.Copy)
-            nc.scalar.activation(out=a_woven[:, :, t], in_=rounded[:].indirect(first_list[:]), func=ACT.Copy)
-        for t in range(2, PACK):
-            nc.vector.tensor_copy(a_woven[:, :, t], a_planes[t][:].indirect(first_list[:]))
-        quantise(a_woven, a_codes, a_scales, slice(0, I))
+            nc.scalar.activation(out=a_picked[:, t, :], in_=rounded[:].indirect(first_list[:]), func=ACT.Copy)
+        nc.vector.tensor_copy(a_picked[:, 2, :], a_planes[2][:].indirect(first_list[:]))
+        for h in range(HALVES):
+            entries = first_list[:, h * (P // 16) : (h + 1) * (P // 16)]
+            nc.vector.tensor_copy(a_picked[:, 3, h * P : (h + 1) * P], a_planes[3][:].indirect(entries))
+        for h in range(HALVES):
+            weave(nc.vector.tensor_copy, a_picked, a_woven, slice(h * P, (h + 1) * P))
+        for h in range(HALVES):
+            quantise(a_woven, a_codes, a_scales, slice(h * P, (h + 1) * P))
         s_ps = [ps.tile([P, 2, I], F32, name="s_ps%d" % b, tag="bank%d" % b) for b in range(2)]
         prob = sb.tile([P, TEAM, I], F32, name="prob")
         for r in range(TEAM):
@@ -123,28 +139,29 @@ def tile_attend_hvpairteams_kernel(tc, taba, dtab, tabb_words, tabb_scales, stak
                 out=prob[:, r, :], in_=s_ps[r // 2][:, r % 2, :], func=ACT.Sigmoid, bias=bias_sb[:, r : r + 1]
             )
 
+        off_centre = sb.tile([P, TEAM, I], F32, name="off_centre")
+        nc.scalar.activation(out=off_centre[:], in_=prob[:], func=ACT.Square, bias=-0.5)
+        nc.scalar.activation(
+            out=warm[:, 1:2], in_=off_centre[:, TEAM - 1, 0:1], func=ACT.Abs_reciprocal_sqrt, bias=1.0
+        )
         d_woven, d_codes, d_scales = operand_tiles("d")
-        for t in range(PACK - 1):
-            nc.vector.tensor_copy(d_woven[:, :, t], d_planes[t][:].indirect(first_list[:]))
+        for t in range(2):
+            nc.vector.tensor_copy(picked[:, t, :], d_planes[t][:].indirect(first_list[:]))
+        nc.vector.tensor_copy(d_woven[:, :, 2], d_planes[2][:].indirect(first_list[:]))
+        nc.vector.tensor_copy(
+            out=d_woven[:, :, 0:2].rearrange("p (c i) t -> p c t i", i=4),
+            in_=picked[:, 0:2, :].rearrange("p t (c i) -> p c t i", i=4),
+        )
 
         stake_ps = ps.tile([P, HALVES, P], F32, name="stake_ps", tag="bank4")
         for h in range(HALVES):
             nc.tensor.transpose(stake_ps[:, h, :], stake_sb[:, h, :], ident[:])
+        stake_turned = sb.tile([P, I], F32, name="stake_turned")
+        nc.scalar.copy(out=stake_turned[:], in_=stake_ps[:].rearrange("p h i -> p (h i)"))
 
-        pairs = sb.tile([P, 2, I], F32, name="pairs")
         chance = sb.tile([P, I], F32, name="chance")
         root = sb.tile([P, I], F32, name="root")
         recip = sb.tile([P, I], F32, name="recip")
-        recip_sq = sb.tile([P, I], F32, name="recip_sq")
-        staked = sb.tile([P, I], F32, name="staked")
-        weight = sb.tile([P, I], F32, name="weight")
-        weight2 = sb.tile([P, I], F32, name="weight2")
-        nc.vector.tensor_tensor(pairs[:], prob[:, 0:2, :], prob[:, 2:4, :], ALU.mult)
-        nc.vector.tensor_tensor(chance[:], pairs[:, 0, :], pairs[:, 1, :], ALU.mult)
-        nc.scalar.activation(out=root[:], in_=chance[:], func=ACT.Abs_reciprocal_sqrt, bias=1.0)
-        nc.scalar.activation(out=recip[:], in_=root[:], func=ACT.Square)
-        nc.scalar.activation(out=recip_sq[:], in_=recip[:], func=ACT.Square)
-        nc.vector.tensor_tensor(staked[:], stake_ps[:].rearrange("p h i -> p (h i)"), chance[:], ALU.mult)
         ts_ps = [ps.tile([P, TEAM, P], F32, name="ts_ps%d" % h, tag="bank%d" % (2 + h)) for h in range(HALVES)]
         for h in range(HALVES):
             cols = slice(h * P, (h + 1) * P)
@@ -155,14 +172,18 @@ def tile_attend_hvpairteams_kernel(tc, taba, dtab, tabb_words, tabb_scales, stak
             quantise(d_woven, d_codes, d_scales, cols)
             for r in range(TEAM):
                 scores(ts_ps[h][:, r, :], r, d_codes, d_scales, cols)
-        nc.vector.tensor_tensor(weight[:], staked[:], recip[:], ALU.mult)
-        nc.vector.tensor_tensor(weight2[:], staked[:], recip_sq[:], ALU.mult)
+        pairs = sb.tile([P, 2, I], F32, name="pairs")
+        for u in range(2):
+            nc.gpsimd.tensor_tensor(pairs[:, u, :], prob[:, 2 * u, :], prob[:, 2 * u + 1, :], ALU.mult)
+        nc.gpsimd.tensor_tensor(chance[:], pairs[:, 0, :], pairs[:, 1, :], ALU.mult)
+        nc.scalar.activation(out=root[:], in_=chance[:], func=ACT.Abs_reciprocal_sqrt, bias=1.0)
+        nc.scalar.activation(out=recip[:], in_=root[:], func=ACT.Square)
 
         moved = []
         sums_back = []
         for h in range(HALVES):
             cols = slice(h * P, (h + 1) * P)
-            moved.append(sb.tile([P, TEAM, P], F32, name="moved%d" % h))
+            moved.append(sb.tile([P, TEAM, P], F32, name="moved%d" % h, tag="moved%d" % h))
             nc.vector.scalar_tensor_tensor(
                 out=moved[h][:], in0=prob[:, :, cols], scalar=1.0, in1=ts_ps[h][:], op0=ALU.subtract, op1=ALU.mult
             )
@@ -176,16 +197,28 @@ def tile_attend_hvpairteams_kernel(tc, taba, dtab, tabb_words, tabb_scales, stak
             sums_back.append(ps.tile([P, P], F32, name="sums_back%d" % h, tag="bank%d" % (7 if h == 0 else 4)))
             nc.tensor.transpose(sums_back[h][:], sums_sb[:], ident[:])
 
+        staked = sb.tile([P, I], F32, name="staked")
+        nc.gpsimd.tensor_tensor(staked[:], stake_turned[:], chance[:], ALU.mult)
         curved = []
         for h in range(HALVES):
             curved.append(sb.tile([P, TEAM, P], F32, name="curved%d" % h))
-            nc.vector.tensor_tensor(curved[h][:], moved[h][:], prob[:, :, h * P : (h + 1) * P], ALU.mult)
+            nc.vector.scalar_tensor_tensor(
+                out=curved[h][:],
+                in0=off_centre[:, :, h * P : (h + 1) * P],
+                scalar=0.25,
+                in1=ts_ps[h][:],
+                op0=ALU.subtract,
+                op1=ALU.mult,
+            )
+        weights = sb.tile([P, 2, I], F32, name="weights")
+        nc.gpsimd.tensor_tensor(weights[:, 0, :], recip[:], staked[:], ALU.mult)
+        nc.gpsimd.tensor_tensor(weights[:, 1, :], recip[:], weights[:, 0, :], ALU.mult)
         out_ps = []
         for h in range(HALVES):
             cols = slice(h * P, (h + 1) * P)
             own = sb.tile([P, TEAM, P], F32, name="own%d" % h)
             nc.vector.tensor_tensor(
-                own[:], curved[h][:], weight[:, cols].unsqueeze(1).to_broadcast([P, TEAM, P]), ALU.mult
+                own[:], curved[h][:], weights[:, 0, cols].unsqueeze(1).to_broadcast([P, TEAM, P]), ALU.mult
             )
             out_ps.append(ps.tile([P, TEAM, G], F32, name="out_ps%d" % h, tag="bank%d" % h))
             for r in range(TEAM):
@@ -196,7 +229,7 @@ def tile_attend_hvpairteams_kernel(tc, taba, dtab, tabb_words, tabb_scales, stak
         for h in range(HALVES):
             cols = slice(h * P, (h + 1) * P)
             team_terms.append(sb.tile([P, P], F32, name="team_term%d" % h))
-            nc.vector.tensor_tensor(team_terms[h][:], sums_back[h][:], weight2[:, cols], ALU.mult)
+            nc.vector.tensor_tensor(team_terms[h][:], sums_back[h][:], weights[:, 1, cols], ALU.mult)
         for h in range(HALVES):
             cols = slice(h * P, (h + 1) * P)
             shared = sb.tile([P, TEAM, P], F32, name="shared%d" % h)
@@ -217,12 +250,13 @@ def tile_attend_hvpairteams_kernel(tc, taba, dtab, tabb_words, tabb_scales, stak
                     start=False,
                     stop=r == TEAM - 1,
                 )
-        for h in range(HALVES):
-            result = sb.tile([P, J], F32, name="result%d" % h)
+        for h, teams in ((0, slice(0, G)), (1, slice(0, G // 2)), (1, slice(G // 2, G))):
+            cols = slice(teams.start * TEAM, teams.stop * TEAM)
+            result = sb.tile([P, cols.stop - cols.start], F32, name="result%d_%d" % (h, teams.start))
             nc.vector.tensor_tensor(
                 result[:].rearrange("p (g r) -> p g r", r=TEAM),
-                out_ps[h][:].rearrange("p r g -> p g r"),
-                base_sb[h][:].rearrange("p (g r) -> p g r", r=TEAM),
+                out_ps[h][:, :, teams].rearrange("p r g -> p g r"),
+                base_sb[h][:, cols].rearrange("p (g r) -> p g r", r=TEAM),
                 ALU.add,
             )
-            nc.sync.dma_start(out=out[h * P : (h + 1) * P, :], in_=result[:])
+            nc.sync.dma_start(out=out[h * P : (h + 1) * P, cols], in_=result[:])

@@ -18,9 +18,18 @@ P = 128
 D, T, U, I, J, G = 512, 1024, 1024, 256, 512, 128
 PACK = 4
 TEAM = 4
-HALVES = 2
+HALVES = I // P
+QUADRANTS = 4
+LIST_ROWS = 16
+LINE_BYTES = 16
+WEAVE_RUN = 4
+SCALAR_PLANES = 2
 
 FLOPS = 2 * 2 * D * I * J
+
+
+def half_columns(h):
+    return slice(h * P, (h + 1) * P)
 
 
 def tile_attend_hvpairteams_kernel(tc, taba, dtab, tabb_words, tabb_scales, stake, bias, base, offs, offs2, out):
@@ -29,8 +38,8 @@ def tile_attend_hvpairteams_kernel(tc, taba, dtab, tabb_words, tabb_scales, stak
         sb = ctx.enter_context(tc.tile_pool(name="sb", bufs=1))
         ps = ctx.enter_context(tc.psum_pool(name="ps", bufs=1))
 
-        first_list = sb.tile([P, I // 16], U16, name="first_list")
-        second_list = sb.tile([P, J // 16], U16, name="second_list")
+        first_list = sb.tile([P, I // LIST_ROWS], U16, name="first_list")
+        second_list = sb.tile([P, J // LIST_ROWS], U16, name="second_list")
         words = sb.tile([P, U], U16, name="words")
         scale_rows = sb.tile([P, U], U8, name="scale_rows")
         a_planes = [sb.tile([P, T], F32, name="a_plane%d" % t) for t in range(PACK)]
@@ -39,12 +48,13 @@ def tile_attend_hvpairteams_kernel(tc, taba, dtab, tabb_words, tabb_scales, stak
         stake_sb = sb.tile([P, HALVES, G], F32, name="stake_sb")
         base_sb = [sb.tile([P, J], F32, name="base_sb%d" % h) for h in range(HALVES)]
         ident = sb.tile([P, P], F32, name="ident")
-        warm = sb.tile([P, 2], F32, name="warm")
+        zero = sb.tile([P, 1], F32, name="zero")
+        one_half = sb.tile([P, 1], F32, name="one_half")
 
         nc.gpsimd.memset(scale_rows[:].bitcast(I32), 0)
         make_identity(nc, ident[:])
-        nc.vector.memset(warm[:, 0:1], 0.0)
-        nc.scalar.activation(out=warm[:, 1:2], in_=warm[:, 0:1], func=ACT.Sigmoid)
+        nc.vector.memset(zero[:], 0.0)
+        nc.scalar.activation(out=one_half[:], in_=zero[:], func=ACT.Sigmoid)
 
         a_rows = taba.rearrange("(p t) c -> p t c", t=PACK)
         d_rows = dtab.rearrange("(p t) c -> p t c", t=PACK)
@@ -52,49 +62,42 @@ def tile_attend_hvpairteams_kernel(tc, taba, dtab, tabb_words, tabb_scales, stak
         nc.sync.dma_start(out=words[:].bitcast(I32), in_=tabb_words[0].bitcast(I32))
         nc.sync.dma_start(first_list[:], offs)
         nc.sync.dma_start(out=a_planes[0][:], in_=a_rows[:, 0, :])
-        for quad in range(4):
+        for quad in range(QUADRANTS):
             nc.sync.dma_start(
                 out=scale_rows[32 * quad : 32 * quad + 4, :].bitcast(I32),
                 in_=tabb_scales[0, 4 * quad : 4 * quad + 4, :].bitcast(I32),
             )
-        nc.sync.dma_start(out=a_planes[1][:], in_=a_rows[:, 1, :])
-        nc.sync.dma_start(out=a_planes[2][:], in_=a_rows[:, 2, :])
-        nc.sync.dma_start(out=a_planes[3][:], in_=a_rows[:, 3, :])
+        for t in range(1, PACK):
+            nc.sync.dma_start(out=a_planes[t][:], in_=a_rows[:, t, :])
         nc.sync.dma_start(out=bias_sb[:], in_=bias.rearrange("o (p r) -> p (o r)", r=TEAM))
-        nc.sync.dma_start(out=d_planes[0][:], in_=d_rows[:, 0, :])
-        nc.sync.dma_start(out=d_planes[1][:], in_=d_rows[:, 1, :])
         nc.sync.dma_start(out=stake_sb[:], in_=stake.rearrange("(h p) g -> p h g", p=P))
-        nc.sync.dma_start(out=d_planes[2][:], in_=d_rows[:, 2, :])
-        nc.sync.dma_start(out=d_planes[3][:], in_=d_rows[:, 3, :])
+        for t in range(PACK):
+            nc.sync.dma_start(out=d_planes[t][:], in_=d_rows[:, t, :])
         for h in range(HALVES):
-            nc.sync.dma_start(out=base_sb[h][:], in_=base[h * P : (h + 1) * P, :])
+            nc.sync.dma_start(out=base_sb[h][:], in_=base[half_columns(h), :])
 
         words_picked = sb.tile([P, J], U16, name="words_picked")
         scales_picked = sb.tile([P, J], U8, name="scales_picked")
         b_words = sb.tile([P, J], U16, name="b_words", align_bytes=64)
         b_scales = sb.tile([P, J], U8, name="b_scales", align_bytes=64)
-        nc.vector.tensor_copy(words_picked[:], words[:].indirect(second_list[:]))
-        nc.vector.tensor_copy(
-            out=b_words[:].rearrange("p (r c g) -> p c r g", r=TEAM, g=8),
-            in_=words_picked[:].rearrange("p (c g r) -> p c r g", r=TEAM, g=8),
-        )
-        nc.vector.tensor_copy(scales_picked[:], scale_rows[:].indirect(second_list[:]))
-        nc.vector.tensor_copy(
-            out=b_scales[:].rearrange("p (r c g) -> p c r g", r=TEAM, g=16),
-            in_=scales_picked[:].rearrange("p (c g r) -> p c r g", r=TEAM, g=16),
-        )
+        for dealt, picked_b, window, run in (
+            (b_words, words_picked, words, LINE_BYTES // 2),
+            (b_scales, scales_picked, scale_rows, LINE_BYTES),
+        ):
+            nc.vector.tensor_copy(picked_b[:], window[:].indirect(second_list[:]))
+            nc.vector.tensor_copy(
+                out=dealt[:].rearrange("p (r c g) -> p c r g", r=TEAM, g=run),
+                in_=picked_b[:].rearrange("p (c g r) -> p c r g", r=TEAM, g=run),
+            )
 
-        def operand_tiles(tag):
-            woven = sb.tile([P, I, PACK], BF16, name=tag + "_woven", tag=tag + "_woven", align_bytes=64)
-            codes = sb.tile([P, I], U32, name=tag + "_codes", tag=tag + "_codes", align_bytes=64)
-            scales = sb.tile([P, I], U8, name=tag + "_scales", align_bytes=64)
+        def operand_tiles(table, woven_tag):
+            woven = sb.tile([P, I, PACK], BF16, name=table + "_woven", tag=woven_tag, align_bytes=64)
+            codes = sb.tile([P, I], U32, name=table + "_codes", align_bytes=64)
+            scales = sb.tile([P, I], U8, name=table + "_scales", align_bytes=64)
             return woven, codes, scales
 
-        def weave(copy, picked, woven, cols):
-            copy(
-                out=woven[:, cols, :].rearrange("p (c i) t -> p c t i", i=4),
-                in_=picked[:, :, cols].rearrange("p t (c i) -> p c t i", i=4),
-            )
+        def half_list(h):
+            return first_list[:, h * (P // LIST_ROWS) : (h + 1) * (P // LIST_ROWS)]
 
         def quantise(woven, codes, scales, cols):
             nc.vector.quantize_mx(
@@ -104,7 +107,7 @@ def tile_attend_hvpairteams_kernel(tc, taba, dtab, tabb_words, tabb_scales, stak
             )
 
         def scores(dst, r, codes, scales, cols):
-            member = slice(r * P, (r + 1) * P)
+            member = slice(r * G, (r + 1) * G)
             nc.tensor.matmul_mx(
                 out=dst,
                 lhsT=b_words[:, member].bitcast(FP4X4),
@@ -115,22 +118,36 @@ def tile_attend_hvpairteams_kernel(tc, taba, dtab, tabb_words, tabb_scales, stak
                 stop=True,
             )
 
-        a_woven, a_codes, a_scales = operand_tiles("a")
-        picked = sb.tile([P, PACK, I], BF16, name="picked")
-        a_picked = picked
-        for t in range(2):
+        def add_turned(dst, src, start, stop):
+            nc.tensor.matmul(dst, lhsT=src, rhs=ident[:], is_transpose=True, start=start, stop=stop)
+
+        a_woven, a_codes, a_scales = operand_tiles("a", "a_woven")
+        a_picked = sb.tile([P, PACK, I], BF16, name="a_picked", tag="a_picked", align_bytes=64)
+        for t in range(SCALAR_PLANES):
             rounded = sb.tile([P, T], BF16, name="a_rounded%d" % t)
             nc.scalar.activation(out=rounded[:], in_=a_planes[t][:], func=ACT.Copy)
             nc.scalar.activation(out=a_picked[:, t, :], in_=rounded[:].indirect(first_list[:]), func=ACT.Copy)
-        nc.vector.tensor_copy(a_picked[:, 2, :], a_planes[2][:].indirect(first_list[:]))
+        for t in range(SCALAR_PLANES, PACK - 1):
+            nc.vector.tensor_copy(a_picked[:, t, :], a_planes[t][:].indirect(first_list[:]))
         for h in range(HALVES):
-            entries = first_list[:, h * (P // 16) : (h + 1) * (P // 16)]
-            nc.vector.tensor_copy(a_picked[:, 3, h * P : (h + 1) * P], a_planes[3][:].indirect(entries))
+            nc.vector.tensor_copy(
+                a_picked[:, PACK - 1, half_columns(h)], a_planes[PACK - 1][:].indirect(half_list(h))
+            )
         for h in range(HALVES):
-            weave(nc.vector.tensor_copy, a_picked, a_woven, slice(h * P, (h + 1) * P))
+            nc.vector.tensor_copy(
+                out=a_woven[:, half_columns(h), :].rearrange("p (c i) t -> p c t i", i=WEAVE_RUN),
+                in_=a_picked[:, :, half_columns(h)].rearrange("p t (c i) -> p c t i", i=WEAVE_RUN),
+            )
         for h in range(HALVES):
-            quantise(a_woven, a_codes, a_scales, slice(h * P, (h + 1) * P))
-        s_ps = [ps.tile([P, 2, I], F32, name="s_ps%d" % b, tag="bank%d" % b) for b in range(2)]
+            quantise(a_woven, a_codes, a_scales, half_columns(h))
+
+        stake_ps = ps.tile([P, HALVES, P], F32, name="stake_ps", tag="bank4")
+        for h in range(HALVES):
+            nc.tensor.transpose(stake_ps[:, h, :], stake_sb[:, h, :], ident[:])
+        stake_turned = sb.tile([P, I], F32, name="stake_turned")
+        nc.scalar.copy(out=stake_turned[:], in_=stake_ps[:].rearrange("p h i -> p (h i)"))
+
+        s_ps = [ps.tile([P, 2, I], F32, name="s_ps%d" % b, tag="bank%d" % b) for b in range(TEAM // 2)]
         prob = sb.tile([P, TEAM, I], F32, name="prob")
         for r in range(TEAM):
             scores(s_ps[r // 2][:, r % 2, :], r, a_codes, a_scales, slice(0, I))
@@ -139,62 +156,56 @@ def tile_attend_hvpairteams_kernel(tc, taba, dtab, tabb_words, tabb_scales, stak
                 out=prob[:, r, :], in_=s_ps[r // 2][:, r % 2, :], func=ACT.Sigmoid, bias=bias_sb[:, r : r + 1]
             )
 
-        off_centre = sb.tile([P, TEAM, I], F32, name="off_centre")
-        nc.scalar.activation(out=off_centre[:], in_=prob[:], func=ACT.Square, bias=-0.5)
+        table_switch = sb.tile([P, 1], F32, name="table_switch")
         nc.scalar.activation(
-            out=warm[:, 1:2], in_=off_centre[:, TEAM - 1, 0:1], func=ACT.Abs_reciprocal_sqrt, bias=1.0
-        )
-        d_woven, d_codes, d_scales = operand_tiles("d")
-        for t in range(2):
-            nc.vector.tensor_copy(picked[:, t, :], d_planes[t][:].indirect(first_list[:]))
-        nc.vector.tensor_copy(d_woven[:, :, 2], d_planes[2][:].indirect(first_list[:]))
-        nc.vector.tensor_copy(
-            out=d_woven[:, :, 0:2].rearrange("p (c i) t -> p c t i", i=4),
-            in_=picked[:, 0:2, :].rearrange("p t (c i) -> p c t i", i=4),
+            out=table_switch[:], in_=prob[:, TEAM - 1, 0:1], func=ACT.Abs_reciprocal_sqrt, bias=1.0
         )
 
-        stake_ps = ps.tile([P, HALVES, P], F32, name="stake_ps", tag="bank4")
-        for h in range(HALVES):
-            nc.tensor.transpose(stake_ps[:, h, :], stake_sb[:, h, :], ident[:])
-        stake_turned = sb.tile([P, I], F32, name="stake_turned")
-        nc.scalar.copy(out=stake_turned[:], in_=stake_ps[:].rearrange("p h i -> p (h i)"))
-
-        chance = sb.tile([P, I], F32, name="chance")
-        root = sb.tile([P, I], F32, name="root")
-        recip = sb.tile([P, I], F32, name="recip")
+        d_woven, d_codes, d_scales = operand_tiles("d", "a_picked")
+        for t in range(PACK - 1):
+            nc.vector.tensor_copy(d_woven[:, :, t], d_planes[t][:].indirect(first_list[:]))
         ts_ps = [ps.tile([P, TEAM, P], F32, name="ts_ps%d" % h, tag="bank%d" % (2 + h)) for h in range(HALVES)]
         for h in range(HALVES):
-            cols = slice(h * P, (h + 1) * P)
-            entries = first_list[:, h * (P // 16) : (h + 1) * (P // 16)]
-            nc.vector.tensor_copy(d_woven[:, cols, PACK - 1], d_planes[PACK - 1][:].indirect(entries))
+            nc.vector.tensor_copy(
+                d_woven[:, half_columns(h), PACK - 1], d_planes[PACK - 1][:].indirect(half_list(h))
+            )
         for h in range(HALVES):
-            cols = slice(h * P, (h + 1) * P)
-            quantise(d_woven, d_codes, d_scales, cols)
+            quantise(d_woven, d_codes, d_scales, half_columns(h))
             for r in range(TEAM):
-                scores(ts_ps[h][:, r, :], r, d_codes, d_scales, cols)
-        pairs = sb.tile([P, 2, I], F32, name="pairs")
-        for u in range(2):
+                scores(ts_ps[h][:, r, :], r, d_codes, d_scales, half_columns(h))
+
+        pairs = sb.tile([P, TEAM // 2, I], F32, name="pairs")
+        chance = sb.tile([P, I], F32, name="chance")
+        root = sb.tile([P, I], F32, name="root", tag="root")
+        recip = sb.tile([P, I], F32, name="recip")
+        for u in range(TEAM // 2):
             nc.gpsimd.tensor_tensor(pairs[:, u, :], prob[:, 2 * u, :], prob[:, 2 * u + 1, :], ALU.mult)
         nc.gpsimd.tensor_tensor(chance[:], pairs[:, 0, :], pairs[:, 1, :], ALU.mult)
         nc.scalar.activation(out=root[:], in_=chance[:], func=ACT.Abs_reciprocal_sqrt, bias=1.0)
         nc.scalar.activation(out=recip[:], in_=root[:], func=ACT.Square)
+        off_centre = sb.tile([P, HALVES, TEAM, P], F32, name="off_centre", tag="root")
+        for h in range(HALVES):
+            nc.scalar.activation(
+                out=off_centre[:, h], in_=prob[:, :, half_columns(h)], func=ACT.Square, scale=-1.0, bias=one_half[:]
+            )
 
-        moved = []
         sums_back = []
         for h in range(HALVES):
-            cols = slice(h * P, (h + 1) * P)
-            moved.append(sb.tile([P, TEAM, P], F32, name="moved%d" % h, tag="moved%d" % h))
+            moved = sb.tile([P, TEAM, P], F32, name="moved%d" % h)
             nc.vector.scalar_tensor_tensor(
-                out=moved[h][:], in0=prob[:, :, cols], scalar=1.0, in1=ts_ps[h][:], op0=ALU.subtract, op1=ALU.mult
+                out=moved[:],
+                in0=prob[:, :, half_columns(h)],
+                scalar=1.0,
+                in1=ts_ps[h][:],
+                op0=ALU.subtract,
+                op1=ALU.mult,
             )
             sums_ps = ps.tile([P, P], F32, name="sums_ps%d" % h, tag="bank%d" % (5 + h))
             for r in range(TEAM):
-                nc.tensor.matmul(
-                    sums_ps[:], lhsT=moved[h][:, r, :], rhs=ident[:], is_transpose=True, start=r == 0, stop=r == TEAM - 1
-                )
+                add_turned(sums_ps[:], moved[:, r, :], start=r == 0, stop=r == TEAM - 1)
             sums_sb = sb.tile([P, P], F32, name="sums_sb%d" % h)
             nc.scalar.copy(out=sums_sb[:], in_=sums_ps[:])
-            sums_back.append(ps.tile([P, P], F32, name="sums_back%d" % h, tag="bank%d" % (7 if h == 0 else 4)))
+            sums_back.append(ps.tile([P, P], F32, name="sums_back%d" % h, tag=("bank7", "bank4")[h]))
             nc.tensor.transpose(sums_back[h][:], sums_sb[:], ident[:])
 
         staked = sb.tile([P, I], F32, name="staked")
@@ -204,52 +215,43 @@ def tile_attend_hvpairteams_kernel(tc, taba, dtab, tabb_words, tabb_scales, stak
             curved.append(sb.tile([P, TEAM, P], F32, name="curved%d" % h))
             nc.vector.scalar_tensor_tensor(
                 out=curved[h][:],
-                in0=off_centre[:, :, h * P : (h + 1) * P],
+                in0=off_centre[:, h],
                 scalar=0.25,
                 in1=ts_ps[h][:],
                 op0=ALU.subtract,
                 op1=ALU.mult,
             )
-        weights = sb.tile([P, 2, I], F32, name="weights")
-        nc.gpsimd.tensor_tensor(weights[:, 0, :], recip[:], staked[:], ALU.mult)
-        nc.gpsimd.tensor_tensor(weights[:, 1, :], recip[:], weights[:, 0, :], ALU.mult)
+        weight = sb.tile([P, I], F32, name="weight")
+        weight_recip = sb.tile([P, I], F32, name="weight_recip")
+        nc.gpsimd.tensor_tensor(weight[:], recip[:], staked[:], ALU.mult)
+        nc.gpsimd.tensor_tensor(weight_recip[:], recip[:], weight[:], ALU.mult)
+
         out_ps = []
         for h in range(HALVES):
-            cols = slice(h * P, (h + 1) * P)
             own = sb.tile([P, TEAM, P], F32, name="own%d" % h)
             nc.vector.tensor_tensor(
-                own[:], curved[h][:], weights[:, 0, cols].unsqueeze(1).to_broadcast([P, TEAM, P]), ALU.mult
+                own[:], curved[h][:], weight[:, half_columns(h)].unsqueeze(1).to_broadcast([P, TEAM, P]), ALU.mult
             )
             out_ps.append(ps.tile([P, TEAM, G], F32, name="out_ps%d" % h, tag="bank%d" % h))
             for r in range(TEAM):
-                nc.tensor.matmul(
-                    out_ps[h][:, r, :], lhsT=own[:, r, :], rhs=ident[:], is_transpose=True, start=r == 0, stop=False
-                )
+                add_turned(out_ps[h][:, r, :], own[:, r, :], start=r == 0, stop=False)
         team_terms = []
         for h in range(HALVES):
-            cols = slice(h * P, (h + 1) * P)
             team_terms.append(sb.tile([P, P], F32, name="team_term%d" % h))
-            nc.vector.tensor_tensor(team_terms[h][:], sums_back[h][:], weights[:, 1, cols], ALU.mult)
+            nc.vector.tensor_tensor(team_terms[h][:], sums_back[h][:], weight_recip[:, half_columns(h)], ALU.mult)
         for h in range(HALVES):
-            cols = slice(h * P, (h + 1) * P)
             shared = sb.tile([P, TEAM, P], F32, name="shared%d" % h)
             nc.vector.scalar_tensor_tensor(
                 out=shared[:],
-                in0=prob[:, :, cols],
+                in0=prob[:, :, half_columns(h)],
                 scalar=1.0,
                 in1=team_terms[h][:].unsqueeze(1).to_broadcast([P, TEAM, P]),
                 op0=ALU.subtract,
                 op1=ALU.mult,
             )
             for r in range(TEAM):
-                nc.tensor.matmul(
-                    out_ps[h][:, r, :],
-                    lhsT=shared[:, r, :],
-                    rhs=ident[:],
-                    is_transpose=True,
-                    start=False,
-                    stop=r == TEAM - 1,
-                )
+                add_turned(out_ps[h][:, r, :], shared[:, r, :], start=False, stop=r == TEAM - 1)
+
         for h, teams in ((0, slice(0, G)), (1, slice(0, G // 2)), (1, slice(G // 2, G))):
             cols = slice(teams.start * TEAM, teams.stop * TEAM)
             result = sb.tile([P, cols.stop - cols.start], F32, name="result%d_%d" % (h, teams.start))
@@ -259,4 +261,4 @@ def tile_attend_hvpairteams_kernel(tc, taba, dtab, tabb_words, tabb_scales, stak
                 base_sb[h][:, cols].rearrange("p (g r) -> p g r", r=TEAM),
                 ALU.add,
             )
-            nc.sync.dma_start(out=out[h * P : (h + 1) * P, cols], in_=result[:])
+            nc.sync.dma_start(out=out[half_columns(h), cols], in_=result[:])

from contextlib import ExitStack

import concourse.mybir as mybir
from concourse.masks import make_identity

F32 = mybir.dt.float32
BF16 = mybir.dt.bfloat16
I32 = mybir.dt.int32
U32 = mybir.dt.uint32
U16 = mybir.dt.uint16
U8 = mybir.dt.uint8
FP8X4 = mybir.dt.float8_e4m3fn_x4
FP4X4 = mybir.dt.float4_e2m1fn_x4
ACT = mybir.ActivationFunctionType
ALU = mybir.AluOpType

P = 128
D, T, U, I, J, G = 512, 1024, 1024, 256, 512, 128
PACK = 4
TEAM = 4
HALVES = I // P
QUADRANTS = 4
LIST_ROWS = 16
LINE_BYTES = 16
WEAVE_RUN = 4
SCALAR_PLANES = 2

FLOPS = 2 * 2 * D * I * J


def half_columns(h):
    return slice(h * P, (h + 1) * P)


def tile_attend_hvpairteams_kernel(tc, taba, dtab, tabb_words, tabb_scales, stake, bias, base, offs, offs2, out):
    nc = tc.nc
    with ExitStack() as ctx:
        sb = ctx.enter_context(tc.tile_pool(name="sb", bufs=1))
        ps = ctx.enter_context(tc.psum_pool(name="ps", bufs=1))

        first_list = sb.tile([P, I // LIST_ROWS], U16, name="first_list")
        second_list = sb.tile([P, J // LIST_ROWS], U16, name="second_list")
        words = sb.tile([P, U], U16, name="words")
        scale_rows = sb.tile([P, U], U8, name="scale_rows")
        a_planes = [sb.tile([P, T], F32, name="a_plane%d" % t) for t in range(PACK)]
        d_planes = [sb.tile([P, T], F32, name="d_plane%d" % t) for t in range(PACK)]
        bias_sb = sb.tile([P, TEAM], F32, name="bias_sb")
        stake_sb = sb.tile([P, HALVES, G], F32, name="stake_sb")
        base_sb = [sb.tile([P, J], F32, name="base_sb%d" % h) for h in range(HALVES)]
        ident = sb.tile([P, P], F32, name="ident")
        zero = sb.tile([P, 1], F32, name="zero")
        one_half = sb.tile([P, 1], F32, name="one_half")

        nc.gpsimd.memset(scale_rows[:].bitcast(I32), 0)
        make_identity(nc, ident[:])
        nc.vector.memset(zero[:], 0.0)
        nc.scalar.activation(out=one_half[:], in_=zero[:], func=ACT.Sigmoid)

        a_rows = taba.rearrange("(p t) c -> p t c", t=PACK)
        d_rows = dtab.rearrange("(p t) c -> p t c", t=PACK)
        nc.sync.dma_start(second_list[:], offs2)
        nc.sync.dma_start(out=words[:].bitcast(I32), in_=tabb_words[0].bitcast(I32))
        nc.sync.dma_start(first_list[:], offs)
        nc.sync.dma_start(out=a_planes[0][:], in_=a_rows[:, 0, :])
        for quad in range(QUADRANTS):
            nc.sync.dma_start(
                out=scale_rows[32 * quad : 32 * quad + 4, :].bitcast(I32),
                in_=tabb_scales[0, 4 * quad : 4 * quad + 4, :].bitcast(I32),
            )
        for t in range(1, PACK):
            nc.sync.dma_start(out=a_planes[t][:], in_=a_rows[:, t, :])
        nc.sync.dma_start(out=bias_sb[:], in_=bias.rearrange("o (p r) -> p (o r)", r=TEAM))
        nc.sync.dma_start(out=stake_sb[:], in_=stake.rearrange("(h p) g -> p h g", p=P))
        for t in range(PACK):
            nc.sync.dma_start(out=d_planes[t][:], in_=d_rows[:, t, :])
        for h in range(HALVES):
            nc.sync.dma_start(out=base_sb[h][:], in_=base[half_columns(h), :])

        words_picked = sb.tile([P, J], U16, name="words_picked")
        scales_picked = sb.tile([P, J], U8, name="scales_picked")
        b_words = sb.tile([P, J], U16, name="b_words", align_bytes=64)
        b_scales = sb.tile([P, J], U8, name="b_scales", align_bytes=64)
        for dealt, picked_b, window, run in (
            (b_words, words_picked, words, LINE_BYTES // 2),
            (b_scales, scales_picked, scale_rows, LINE_BYTES),
        ):
            nc.vector.tensor_copy(picked_b[:], window[:].indirect(second_list[:]))
            nc.vector.tensor_copy(
                out=dealt[:].rearrange("p (r c g) -> p c r g", r=TEAM, g=run),
                in_=picked_b[:].rearrange("p (c g r) -> p c r g", r=TEAM, g=run),
            )

        def operand_tiles(table, woven_tag):
            woven = sb.tile([P, I, PACK], BF16, name=table + "_woven", tag=woven_tag, align_bytes=64)
            codes = sb.tile([P, I], U32, name=table + "_codes", align_bytes=64)
            scales = sb.tile([P, I], U8, name=table + "_scales", align_bytes=64)
            return woven, codes, scales

        def half_list(h):
            return first_list[:, h * (P // LIST_ROWS) : (h + 1) * (P // LIST_ROWS)]

        def quantise(woven, codes, scales, cols):
            nc.vector.quantize_mx(
                out=codes[:, cols].bitcast(FP8X4),
                scales=scales[:, cols],
                in_=woven[:, cols, :].rearrange("p i t -> p (i t)"),
            )

        def scores(dst, r, codes, scales, cols):
            member = slice(r * G, (r + 1) * G)
            nc.tensor.matmul_mx(
                out=dst,
                lhsT=b_words[:, member].bitcast(FP4X4),
                lhsT_scale=b_scales[:, member],
                rhs=codes[:, cols].bitcast(FP8X4),
                rhs_scale=scales[:, cols],
                start=True,
                stop=True,
            )

        def add_turned(dst, src, start, stop):
            nc.tensor.matmul(dst, lhsT=src, rhs=ident[:], is_transpose=True, start=start, stop=stop)

        a_woven, a_codes, a_scales = operand_tiles("a", "a_woven")
        a_picked = sb.tile([P, PACK, I], BF16, name="a_picked", tag="a_picked", align_bytes=64)
        for t in range(SCALAR_PLANES):
            rounded = sb.tile([P, T], BF16, name="a_rounded%d" % t)
            nc.scalar.activation(out=rounded[:], in_=a_planes[t][:], func=ACT.Copy)
            nc.scalar.activation(out=a_picked[:, t, :], in_=rounded[:].indirect(first_list[:]), func=ACT.Copy)
        for t in range(SCALAR_PLANES, PACK - 1):
            nc.vector.tensor_copy(a_picked[:, t, :], a_planes[t][:].indirect(first_list[:]))
        for h in range(HALVES):
            nc.vector.tensor_copy(
                a_picked[:, PACK - 1, half_columns(h)], a_planes[PACK - 1][:].indirect(half_list(h))
            )
        for h in range(HALVES):
            nc.vector.tensor_copy(
                out=a_woven[:, half_columns(h), :].rearrange("p (c i) t -> p c t i", i=WEAVE_RUN),
                in_=a_picked[:, :, half_columns(h)].rearrange("p t (c i) -> p c t i", i=WEAVE_RUN),
            )
        for h in range(HALVES):
            quantise(a_woven, a_codes, a_scales, half_columns(h))

        stake_ps = ps.tile([P, HALVES, P], F32, name="stake_ps", tag="bank4")
        for h in range(HALVES):
            nc.tensor.transpose(stake_ps[:, h, :], stake_sb[:, h, :], ident[:])
        stake_turned = sb.tile([P, I], F32, name="stake_turned")
        nc.scalar.copy(out=stake_turned[:], in_=stake_ps[:].rearrange("p h i -> p (h i)"))

        s_ps = [ps.tile([P, 2, I], F32, name="s_ps%d" % b, tag="bank%d" % b) for b in range(TEAM // 2)]
        prob = sb.tile([P, TEAM, I], F32, name="prob")
        for r in range(TEAM):
            scores(s_ps[r // 2][:, r % 2, :], r, a_codes, a_scales, slice(0, I))
        for r in range(TEAM):
            nc.scalar.activation(
                out=prob[:, r, :], in_=s_ps[r // 2][:, r % 2, :], func=ACT.Sigmoid, bias=bias_sb[:, r : r + 1]
            )

        table_switch = sb.tile([P, 1], F32, name="table_switch")
        nc.scalar.activation(
            out=table_switch[:], in_=prob[:, TEAM - 1, 0:1], func=ACT.Abs_reciprocal_sqrt, bias=1.0
        )

        d_woven, d_codes, d_scales = operand_tiles("d", "a_picked")
        for t in range(PACK - 1):
            nc.vector.tensor_copy(d_woven[:, :, t], d_planes[t][:].indirect(first_list[:]))
        ts_ps = [ps.tile([P, TEAM, P], F32, name="ts_ps%d" % h, tag="bank%d" % (2 + h)) for h in range(HALVES)]
        for h in range(HALVES):
            nc.vector.tensor_copy(
                d_woven[:, half_columns(h), PACK - 1], d_planes[PACK - 1][:].indirect(half_list(h))
            )
        for h in range(HALVES):
            quantise(d_woven, d_codes, d_scales, half_columns(h))
            for r in range(TEAM):
                scores(ts_ps[h][:, r, :], r, d_codes, d_scales, half_columns(h))

        pairs = sb.tile([P, TEAM // 2, I], F32, name="pairs")
        chance = sb.tile([P, I], F32, name="chance")
        root = sb.tile([P, I], F32, name="root", tag="root")
        recip = sb.tile([P, I], F32, name="recip")
        for u in range(TEAM // 2):
            nc.gpsimd.tensor_tensor(pairs[:, u, :], prob[:, 2 * u, :], prob[:, 2 * u + 1, :], ALU.mult)
        nc.gpsimd.tensor_tensor(chance[:], pairs[:, 0, :], pairs[:, 1, :], ALU.mult)
        nc.scalar.activation(out=root[:], in_=chance[:], func=ACT.Abs_reciprocal_sqrt, bias=1.0)
        nc.scalar.activation(out=recip[:], in_=root[:], func=ACT.Square)
        off_centre = sb.tile([P, HALVES, TEAM, P], F32, name="off_centre", tag="root")
        for h in range(HALVES):
            nc.scalar.activation(
                out=off_centre[:, h], in_=prob[:, :, half_columns(h)], func=ACT.Square, scale=-1.0, bias=one_half[:]
            )

        sums_back = []
        for h in range(HALVES):
            moved = sb.tile([P, TEAM, P], F32, name="moved%d" % h)
            nc.vector.scalar_tensor_tensor(
                out=moved[:],
                in0=prob[:, :, half_columns(h)],
                scalar=1.0,
                in1=ts_ps[h][:],
                op0=ALU.subtract,
                op1=ALU.mult,
            )
            sums_ps = ps.tile([P, P], F32, name="sums_ps%d" % h, tag="bank%d" % (5 + h))
            for r in range(TEAM):
                add_turned(sums_ps[:], moved[:, r, :], start=r == 0, stop=r == TEAM - 1)
            sums_sb = sb.tile([P, P], F32, name="sums_sb%d" % h)
            nc.scalar.copy(out=sums_sb[:], in_=sums_ps[:])
            sums_back.append(ps.tile([P, P], F32, name="sums_back%d" % h, tag=("bank7", "bank4")[h]))
            nc.tensor.transpose(sums_back[h][:], sums_sb[:], ident[:])

        staked = sb.tile([P, I], F32, name="staked")
        nc.gpsimd.tensor_tensor(staked[:], stake_turned[:], chance[:], ALU.mult)
        curved = []
        for h in range(HALVES):
            curved.append(sb.tile([P, TEAM, P], F32, name="curved%d" % h))
            nc.vector.scalar_tensor_tensor(
                out=curved[h][:],
                in0=off_centre[:, h],
                scalar=0.25,
                in1=ts_ps[h][:],
                op0=ALU.subtract,
                op1=ALU.mult,
            )
        weight = sb.tile([P, I], F32, name="weight")
        weight_recip = sb.tile([P, I], F32, name="weight_recip")
        nc.gpsimd.tensor_tensor(weight[:], recip[:], staked[:], ALU.mult)
        nc.gpsimd.tensor_tensor(weight_recip[:], recip[:], weight[:], ALU.mult)

        out_ps = []
        for h in range(HALVES):
            own = sb.tile([P, TEAM, P], F32, name="own%d" % h)
            nc.vector.tensor_tensor(
                own[:], curved[h][:], weight[:, half_columns(h)].unsqueeze(1).to_broadcast([P, TEAM, P]), ALU.mult
            )
            out_ps.append(ps.tile([P, TEAM, G], F32, name="out_ps%d" % h, tag="bank%d" % h))
            for r in range(TEAM):
                add_turned(out_ps[h][:, r, :], own[:, r, :], start=r == 0, stop=False)
        team_terms = []
        for h in range(HALVES):
            team_terms.append(sb.tile([P, P], F32, name="team_term%d" % h))
            nc.vector.tensor_tensor(team_terms[h][:], sums_back[h][:], weight_recip[:, half_columns(h)], ALU.mult)
        for h in range(HALVES):
            shared = sb.tile([P, TEAM, P], F32, name="shared%d" % h)
            nc.vector.scalar_tensor_tensor(
                out=shared[:],
                in0=prob[:, :, half_columns(h)],
                scalar=1.0,
                in1=team_terms[h][:].unsqueeze(1).to_broadcast([P, TEAM, P]),
                op0=ALU.subtract,
                op1=ALU.mult,
            )
            for r in range(TEAM):
                add_turned(out_ps[h][:, r, :], shared[:, r, :], start=False, stop=r == TEAM - 1)

        for h, teams in ((0, slice(0, G)), (1, slice(0, G // 2)), (1, slice(G // 2, G))):
            cols = slice(teams.start * TEAM, teams.stop * TEAM)
            result = sb.tile([P, cols.stop - cols.start], F32, name="result%d_%d" % (h, teams.start))
            nc.vector.tensor_tensor(
                result[:].rearrange("p (g r) -> p g r", r=TEAM),
                out_ps[h][:, :, teams].rearrange("p r g -> p g r"),
                base_sb[h][:, cols].rearrange("p (g r) -> p g r", r=TEAM),
                ALU.add,
            )
            nc.sync.dma_start(out=out[half_columns(h), cols], in_=result[:])
